import numpy as np
import ml_dtypes


def mxq(x, axis, fmt="e4m3"):
    dtype, down = {"e4m3": (ml_dtypes.float8_e4m3fn, 7), "e5m2": (ml_dtypes.float8_e5m2, 14)}[fmt]
    v = np.moveaxis(np.asarray(x, np.float32).astype(ml_dtypes.bfloat16).astype(np.float64), axis, -1)
    blocks = v.reshape(v.shape[:-1] + (-1, 32))
    amax = np.abs(blocks).max(-1, keepdims=True)
    byte = np.maximum(np.where(amax > 0, np.frexp(amax)[1] - 1 + 127, 0) - down, 1)
    scale = np.exp2(byte - 127.0)
    codes = (blocks / scale).astype(np.float32).astype(dtype).astype(np.float64)
    return np.moveaxis((codes * scale).reshape(v.shape), -1, axis)


WIDE = False


def mx_kscale(k):
    if not WIDE:
        return np.ones(k)
    levels = np.array([10, -10, 5, -5, 0])
    if k % 512:
        return np.exp2(np.random.permutation(np.resize(levels, k // 32))).repeat(32)
    a = np.empty((k // 512, 16))
    for p in range(k // 512):
        a[p, :8] = np.random.permutation(np.resize(levels, 8))
        for g in range(8):
            far = levels[np.abs(levels - a[p, g]) >= 10]
            a[p, g + 8] = far[np.random.randint(len(far))]
    return np.exp2(a.ravel()).repeat(32)


BF16 = ml_dtypes.bfloat16


def bf(x):
    return np.asarray(x, np.float32).astype(BF16)


def f64(x):
    return np.asarray(x).astype(np.float64)


E2M1 = np.array([0.0, 0.5, 1.0, 1.5, 2.0, 3.0, 4.0, 6.0, -0.0, -0.5, -1.0, -1.5, -2.0, -3.0, -4.0, -6.0])


def pack_weight(w, fmt):
    k, n = w.shape
    w = f64(bf(w)).reshape(k // 32, 32, n)
    amax = np.abs(w).max(1)
    if fmt == "e4m3":
        byte = np.frexp(amax)[1] - 1 + 127 - 7
    else:
        mant, ex = np.frexp(amax / 6.0)
        byte = np.where(mant > 0.5, ex, ex - 1) + 127
    byte = np.clip(np.where(amax > 0, byte, 1), 1, 254)
    scaled = (w * np.exp2(127.0 - byte)[:, None, :]).reshape(k, n).astype(np.float32)
    by_word = np.ascontiguousarray(scaled.reshape(k // 512, 128, 4, n).transpose(0, 1, 3, 2))
    if fmt == "e4m3":
        words = by_word.astype(ml_dtypes.float8_e4m3fn).view(np.uint8)
    else:
        c = by_word.astype(ml_dtypes.float4_e2m1fn).view(np.uint8) & 0xF
        words = c[..., 0::2] | (c[..., 1::2] << 4)
    return np.ascontiguousarray(words), np.ascontiguousarray(byte.astype(np.uint8).reshape(k // 512, 16, n))


def unpack_weight(words, scales, fmt):
    g, p, n, _ = words.shape
    if fmt == "e4m3":
        vals = np.ascontiguousarray(words).view(ml_dtypes.float8_e4m3fn).astype(np.float64)
    else:
        nib = np.empty((g, p, n, 4), np.uint8)
        nib[..., 0::2] = words & 0xF
        nib[..., 1::2] = words >> 4
        vals = E2M1[nib]
    vals = vals * np.repeat(np.exp2(scales.astype(np.float64) - 127.0), 8, axis=1)[..., None]
    return vals.transpose(0, 1, 3, 2).reshape(g * 512, n)
def pack4(w):
    words, scales = pack_weight(w, "e2m1")
    return words.reshape(words.shape[0], 128, -1), scales


def unpack4(words, scales):
    return unpack_weight(words.reshape(words.shape[0], 128, -1, 2), scales, "e2m1")


def planes(Y):
    n, m = Y.shape
    b = f64(bf(Y)).reshape(n // 32, 32, m)
    amax = np.abs(b).max(1)
    byte = np.clip(np.where(amax > 0, np.frexp(amax)[1] - 1 + 127 - 7, 1), 1, 254)
    codes = (b * np.exp2(127.0 - byte)[:, None, :]).reshape(n, m).astype(np.float32).astype(ml_dtypes.float8_e4m3fn).view(np.uint8)
    words = codes.reshape(n // 512, 128, 4, m).transpose(0, 1, 3, 2)
    return np.ascontiguousarray(words), np.ascontiguousarray(byte.astype(np.uint8).reshape(n // 512, 16, m))


B, T, R, D, K = 2, 512, 1024, 1024, 1024


def setup_inputs():
    s, t = mx_kscale(R), mx_kscale(D)
    h = bf(np.random.standard_normal((B, T, R)) * s)
    wa = bf(np.random.standard_normal(R) * 0.7 / np.sqrt(R) / s)
    wb_words, wb_scales = pack4(np.random.standard_normal((R, D)) / np.sqrt(R) / s[:, None])
    bb = bf(0.3 * np.random.standard_normal(D))
    wy = bf(np.random.standard_normal(D) * t)
    wemb_words, wemb_scales = pack4(np.random.standard_normal((D, K)) / np.sqrt(D) / t[:, None])
    x = bf(np.random.uniform(0.0, 2.0, (B, T, K)))
    return {
        "h": h,
        "wa": wa,
        "wb_words": wb_words,
        "wb_scales": wb_scales,
        "bb": bb,
        "wy": wy,
        "wemb_words": wemb_words,
        "wemb_scales": wemb_scales,
        "x": x,
    }


def visit_attention(h, wa):
    e = np.sum(h * wa, axis=-1)
    p = np.exp(e - e.max(axis=1, keepdims=True))
    return p / p.sum(axis=1, keepdims=True)


def code_coefficients(h, wb, bb, wy, wemb):
    beta = np.tanh((mxq(h, 2, "e4m3") @ wb) + bb)
    u = beta * wy
    return mxq(u, 2, "e4m3") @ wemb


def core(h, wa, wb_words, wb_scales, bb, wy, wemb_words, wemb_scales, x):
    num_visits = h.shape[1]
    alpha = visit_attention(f64(h), f64(wa))
    wb = unpack4(wb_words, wb_scales)
    wemb = unpack4(wemb_words, wemb_scales)
    c = code_coefficients(f64(h), wb, f64(bb), f64(wy), wemb)
    omega = num_visits * alpha[:, :, None] * c * f64(x)
    return omega


def reference(h, wa, wb_words, wb_scales, bb, wy, wemb_words, wemb_scales, x):
    R_out = core(h, wa, wb_words, wb_scales, bb, wy, wemb_words, wemb_scales, x)
    words, scales = planes(np.moveaxis(R_out, 1, 0).reshape(512, -1))
    return R_out, words, scales

@@ -1,0 +1,489 @@
+from contextlib import ExitStack
+
+import concourse.mybir as mybir
+from concourse.masks import make_identity
+
+B, T, R, D, K = 2, 512, 1024, 1024, 1024
+FLOPS = 2 * B * T * R * D + 2 * B * T * D * K + 2 * B * T * R
+
+F32 = mybir.dt.float32
+BF16 = mybir.dt.bfloat16
+I32 = mybir.dt.int32
+U32 = mybir.dt.uint32
+U16 = mybir.dt.uint16
+U8 = mybir.dt.uint8
+FP8X4 = mybir.dt.float8_e4m3fn_x4
+FP4X4 = mybir.dt.float4_e2m1fn_x4
+ALU = mybir.AluOpType
+ACT = mybir.ActivationFunctionType
+AX = mybir.AxisListType
+
+P = 128
+PACK = 4
+PASSES = 2
+BANK = 512
+SCALAR_BANKS = 4
+VECTOR_BANKS = 3
+RUN = 4
+
+
+def tile_retaincodecontributionmap_x2_kernel(
+    tc, h, wa, wb_words, wb_scales, bb, wy, wemb_words, wemb_scales, x, out_0, out_1, out_2
+):
+    nc = tc.nc
+    with ExitStack() as ctx:
+        sb = ctx.enter_context(tc.tile_pool(name="sb", bufs=1))
+        ps = ctx.enter_context(tc.psum_pool(name="ps", bufs=1))
+        ctx.enter_context(tc.manual_schedule())
+
+        def sbuf(name, shape, dtype):
+            return sb.tile(shape, dtype, name=name, align_bytes=256)
+
+        bank_count = {"scalar": 0, "vector": 0}
+
+        def next_bank(reader, banks):
+            n = bank_count[reader]
+            bank_count[reader] = n + 1
+            return ps.tile([P, BANK], F32, name="%s_bank_%d" % (reader, n), tag="%s_bank_%d" % (reader, n % banks))
+
+        chunks = [(0, 0, 2), (0, 2, 2), (1, 0, 2), (1, 2, 2)]
+
+        def chunk_of(b, s):
+            return [c for c, (cb, s0, ns) in enumerate(chunks) if cb == b and s0 <= s < s0 + ns][0]
+
+        ident = sbuf("ident", [P, P], F32)
+        own_m = sbuf("own_m", [P, 32], F32)
+        pick = sbuf("pick", [P, 4, 32], F32)
+        own_q = sbuf("own_q", [P, 4], F32)
+        own_t = sbuf("own_t", [P, PACK], F32)
+        neg_own_t = sbuf("neg_own_t", [P, PACK], F32)
+        inv_visits = sbuf("inv_visits", [P, 2], F32)
+        h_loads = [[(0, 1), (1, 1), (2, 2)], [(0, 2), (2, 2)]]
+        h_sb = [[sbuf("h_%d_%d" % (b, s0), [P, ns, R], BF16) for (s0, ns) in h_loads[b]] for b in range(B)]
+        x_sb = [sbuf("x_%d" % b, [P, PACK, K], BF16) for b in range(B)]
+        wb_raw = [sbuf("wb_raw_%d" % j, [P, PASSES, 2 * BANK], U8) for j in range(PASSES)]
+        wb_dealt = [sbuf("wb_dealt_%d" % j, [P, PASSES, 2 * BANK], U8) for j in range(PASSES)]
+        wbs_raw = sbuf("wbs_raw", [P, PASSES, D], U8)
+        wbs_dealt = [sbuf("wbs_dealt_%d" % j, [P, PASSES, BANK], U8) for j in range(PASSES)]
+        we_sb = sbuf("we_sb", [P, PASSES, 2 * K], U8)
+        wes_sb = sbuf("wes_sb", [P, PASSES, K], U8)
+        wa_sb = sbuf("wa_sb", [P, PASSES, PACK], BF16)
+        bb_sb = sbuf("bb_sb", [P, PASSES, PACK], BF16)
+        wy_sb = sbuf("wy_sb", [P, PASSES, PACK], BF16)
+        ht = [sbuf("ht_%d" % c, [P, PASSES, P * ns * PACK], BF16) for c, (b, s0, ns) in enumerate(chunks)]
+        h_codes = [sbuf("h_codes_%d" % c, [P, PASSES, P * ns], U32) for c, (b, s0, ns) in enumerate(chunks)]
+        h_scales = [sbuf("h_scales_%d" % c, [P, PASSES, P * ns], U8) for c, (b, s0, ns) in enumerate(chunks)]
+        beta = [[sbuf("beta_%d_%d" % (c, j), [P, PACK, P * ns], F32) for j in range(PASSES)]
+                for c, (b, s0, ns) in enumerate(chunks)]
+        u_bf = [[[sbuf("u_%d_%d_%d" % (b, i, j), [P, 2 * P * PACK], BF16) for j in range(PASSES)] for i in range(2)]
+                for b in range(B)]
+        u_codes = [[[sbuf("uc_%d_%d_%d" % (b, i, j), [P, 2 * P], U32) for j in range(PASSES)] for i in range(2)]
+                   for b in range(B)]
+        u_scales = [[[sbuf("us_%d_%d_%d" % (b, i, j), [P, 2 * P], U8) for j in range(PASSES)] for i in range(2)]
+                    for b in range(B)]
+        ranges = [[(0, 512), (512, 512)], [(0, 512), (512, 256), (768, 256)]]
+        res = [[sbuf("res_%d_%d" % (b, k0), [P, PACK, n], F32) for (k0, n) in ranges[b]] for b in range(B)]
+        res_bf = [[sbuf("resbf_%d_%d" % (b, k0), [P, n * PACK], BF16) for (k0, n) in ranges[b]] for b in range(B)]
+        res_codes = [[sbuf("resc_%d_%d" % (b, k0), [P, n], U32) for (k0, n) in ranges[b]] for b in range(B)]
+        res_scales = sbuf("res_scales", [P, B * K], U8)
+        masked = [sbuf("masked_%d" % b, [P, 16, PACK], F32) for b in range(B)]
+        part = [sbuf("part_%d" % b, [P, PACK, 4], F32) for b in range(B)]
+        row_min = [sbuf("row_min_%d" % b, [P, 1], F32) for b in range(B)]
+        all_min = [sbuf("all_min_%d" % b, [P, 1], F32) for b in range(B)]
+        expo = [sbuf("expo_%d" % b, [P, PACK, 4], F32) for b in range(B)]
+        kept = [sbuf("kept_%d" % b, [P, PACK, 4], F32) for b in range(B)]
+        row_sum = [sbuf("row_sum_%d" % b, [P, 1], F32) for b in range(B)]
+        factor = [sbuf("factor_%d" % b, [P, 1], F32) for b in range(B)]
+        alpha = [sbuf("alpha_%d" % b, [P, PACK], F32) for b in range(B)]
+        small = {0: ps.tile([P, BANK], F32, name="small", tag="small")}
+
+        def small_cols(b, c0, n):
+            if b not in small:
+                small[b] = next_bank("scalar", SCALAR_BANKS)
+            return small[b][:, c0 : c0 + n]
+
+        def load_h(b, i):
+            s0, ns = h_loads[b][i]
+            nc.sync.dma_start(out=h_sb[b][i][:], in_=h[b].rearrange("(p s) r -> p s r", s=PACK)[:, s0 : s0 + ns, :])
+
+        def load_scale_rows(dst, src):
+            for q in range(4):
+                nc.sync.dma_start(
+                    out=dst[32 * q : 32 * q + 4, :, :].bitcast(I32),
+                    in_=src[:, 4 * q : 4 * q + 4, :].rearrange("g r n -> r g n").bitcast(I32),
+                )
+
+        def load_wb(j):
+            nc.sync.dma_start(
+                out=wb_raw[j][:].bitcast(I32),
+                in_=wb_words[:, :, 2 * BANK * j : 2 * BANK * (j + 1)].rearrange("g p n -> p g n").bitcast(I32),
+            )
+
+        def load_vec(dst, src):
+            nc.sync.dma_start(out=dst[:], in_=src.rearrange("(g p t) -> p g t", g=PASSES, t=PACK))
+
+        nc.vector.memset(wbs_raw[:].bitcast(I32), 0)
+        make_identity(nc, ident[:])
+        load_h(0, 0)
+        load_h(0, 1)
+        load_vec(wa_sb, wa)
+        load_scale_rows(wbs_raw, wb_scales)
+        load_h(0, 2)
+        load_wb(0)
+        load_wb(1)
+        load_vec(bb_sb, bb)
+        load_vec(wy_sb, wy)
+        load_h(1, 0)
+        load_h(1, 1)
+        nc.sync.dma_start(out=we_sb[:].bitcast(I32), in_=wemb_words.rearrange("g p n -> p g n").bitcast(I32))
+        load_scale_rows(wes_sb, wemb_scales)
+        for b in range(B):
+            nc.sync.dma_start(out=x_sb[b][:], in_=x[b].rearrange("(p s) k -> p s k", s=PACK))
+
+        nc.vector.memset(inv_visits[:], 1.0 / (4 * T))
+        nc.vector.tensor_reduce(out=own_t[:], in_=ident[:].rearrange("p (m t) -> p t m", t=PACK), axis=AX.X, op=ALU.add)
+        nc.vector.tensor_reduce(out=own_m[:], in_=ident[:].rearrange("p (m t) -> p m t", t=PACK), axis=AX.X, op=ALU.add)
+        nc.vector.tensor_reduce(out=own_q[:], in_=ident[:].rearrange("p (q m) -> p q m", q=4), axis=AX.X, op=ALU.add)
+        nc.vector.tensor_copy(out=pick[:], in_=own_m[:].unsqueeze(1).to_broadcast([P, 4, 32]))
+        nc.vector.tensor_scalar(out=neg_own_t[:], in0=own_t[:], scalar1=-1.0, scalar2=None, op0=ALU.mult)
+
+        def deal_scales(j):
+            nc.vector.tensor_copy(
+                out=wbs_dealt[j][:].rearrange("p g (t m) -> p g t m", t=PACK),
+                in_=wbs_raw[:, :, BANK * j : BANK * (j + 1)].rearrange("p g (m t) -> p g t m", t=PACK),
+            )
+
+        def deal_words(j):
+            nc.vector.tensor_copy(
+                out=wb_dealt[j][:].bitcast(U16).rearrange("p g (t m) -> p g t m", t=PACK),
+                in_=wb_raw[j][:].bitcast(U16).rearrange("p g (m t) -> p g t m", t=PACK),
+            )
+
+        turned = {}
+
+        def turn_h(b, s):
+            bank = next_bank("scalar", SCALAR_BANKS)
+            i = [n for n, (s0, ns) in enumerate(h_loads[b]) if s0 <= s][-1]
+            words = h_sb[b][i][:, s - h_loads[b][i][0], :].bitcast(F32)
+            for g in range(PASSES):
+                for u in range(2):
+                    col = P * (2 * g + u)
+                    nc.tensor.transpose(bank[:, col : col + P], words[:, 256 * g + u : 256 * (g + 1) : 2], ident[:])
+            turned[(b, s)] = bank
+
+        def copy_ht(b, s):
+            c = chunk_of(b, s)
+            ls = s - chunks[c][1]
+            dst = ht[c][:].bitcast(F32)[:, :, 2 * P * ls : 2 * P * (ls + 1)]
+            nc.scalar.copy(
+                out=dst.rearrange("p g (m u) -> p g m u", u=2),
+                in_=turned[(b, s)][:].rearrange("p (g u m) -> p g m u", g=PASSES, u=2),
+            )
+
+        def quantize_h(c, gs):
+            nc.vector.quantize_mx(
+                out=h_codes[c][:, gs, :].rearrange("p g n -> p (g n)").bitcast(FP8X4),
+                scales=h_scales[c][:, gs, :].rearrange("p g n -> p (g n)"),
+                in_=ht[c][:, gs, :].rearrange("p g n -> p (g n)"),
+            )
+
+        def score_products(b, s):
+            c = chunk_of(b, s)
+            ls = s - chunks[c][1]
+            for q in range(4):
+                for g in range(PASSES):
+                    col = P * (4 * ls + q)
+                    nc.tensor.matmul(
+                        small_cols(b, 16 * s + 4 * q, PACK),
+                        lhsT=ht[c][:, g, col : col + P],
+                        rhs=wa_sb[:, g, :],
+                        start=(g == 0),
+                        stop=(g == PASSES - 1),
+                    )
+
+        def score_mask(b):
+            nc.vector.tensor_tensor(
+                out=masked[b][:],
+                in0=small_cols(b, 0, 64).rearrange("p (c t) -> p c t", t=PACK),
+                in1=neg_own_t[:].unsqueeze(1).to_broadcast([P, 16, PACK]),
+                op=ALU.mult,
+            )
+
+        def score_partial(b):
+            nc.vector.tensor_reduce(
+                out=part[b][:].rearrange("p s q -> p (s q)"), in_=masked[b][:], axis=AX.X, op=ALU.add
+            )
+
+        def score_gather(b):
+            nc.tensor.matmul(
+                small_cols(b, 64, 16),
+                lhsT=pick[:].rearrange("p q m -> p (q m)"),
+                rhs=part[b][:].rearrange("p s q -> p (s q)"),
+                start=True,
+                stop=True,
+            )
+
+        def score_row_min(b):
+            nc.vector.tensor_reduce(out=row_min[b][:], in_=small_cols(b, 64, 16), axis=AX.X, op=ALU.min)
+
+        def score_spread_min(b):
+            nc.tensor.transpose(small_cols(b, 128, P), row_min[b][:].to_broadcast([P, P]), ident[:])
+
+        def score_all_min(b):
+            nc.vector.tensor_reduce(out=all_min[b][:], in_=small_cols(b, 128, P), axis=AX.X, op=ALU.min)
+
+        def score_exp(b):
+            nc.scalar.activation(
+                out=expo[b][:].rearrange("p s q -> p (s q)"), in_=small_cols(b, 64, 16), func=ACT.Exp, bias=all_min[b][:], scale=-1.0,
+                accum_out=row_sum[b][:],
+            )
+
+        def score_total(b):
+            nc.tensor.matmul(
+                small_cols(b, 80, 2), lhsT=row_sum[b][:].to_broadcast([P, P]), rhs=inv_visits[:], start=True, stop=True
+            )
+
+        def score_factor(b):
+            nc.vector.reciprocal(out=factor[b][:], in_=small_cols(b, 80, 1))
+
+        def score_keep(b):
+            nc.vector.scalar_tensor_tensor(
+                out=kept[b][:], in0=expo[b][:], scalar=factor[b][:],
+                in1=own_q[:].unsqueeze(1).to_broadcast([P, PACK, 4]), op0=ALU.mult, op1=ALU.mult,
+            )
+
+        def score_alpha(b):
+            nc.vector.tensor_reduce(out=alpha[b][:], in_=kept[b][:], axis=AX.X, op=ALU.add)
+
+        pre = {}
+
+        def stage1(c, j, ts):
+            n = h_codes[c].shape[2]
+            bank = next_bank("scalar", SCALAR_BANKS)
+            for i, t in enumerate(ts):
+                for g in range(PASSES):
+                    nc.tensor.matmul_mx(
+                        out=bank[:, n * i : n * (i + 1)],
+                        lhsT=wb_dealt[j][:, g, 2 * P * t : 2 * P * (t + 1)].bitcast(FP4X4),
+                        lhsT_scale=wbs_dealt[j][:, g, P * t : P * (t + 1)],
+                        rhs=h_codes[c][:, g, :].bitcast(FP8X4),
+                        rhs_scale=h_scales[c][:, g, :],
+                        start=(g == 0),
+                        stop=(g == PASSES - 1),
+                    )
+                pre[(c, j, t)] = bank[:, n * i : n * (i + 1)]
+
+        def tanh(c, j, ts):
+            for t in ts:
+                nc.scalar.activation(
+                    out=beta[c][j][:, t, :], in_=pre[(c, j, t)], func=ACT.Tanh, bias=bb_sb[:, j, t : t + 1]
+                )
+
+        def make_u(b, i, j):
+            c = chunk_of(b, 2 * i)
+            m0 = P * (2 * i - chunks[c][1])
+            groups = 2 * P // RUN
+            nc.vector.tensor_tensor(
+                out=u_bf[b][i][j][:].rearrange("p (c i t) -> p c t i", i=RUN, t=PACK),
+                in0=beta[c][j][:, :, m0 : m0 + 2 * P].rearrange("p t (c i) -> p c t i", i=RUN),
+                in1=wy_sb[:, j, :].unsqueeze(1).unsqueeze(3).to_broadcast([P, groups, PACK, RUN]),
+                op=ALU.mult,
+            )
+
+        def quantize_u(b, i, j):
+            nc.vector.quantize_mx(out=u_codes[b][i][j][:].bitcast(FP8X4), scales=u_scales[b][i][j][:], in_=u_bf[b][i][j][:])
+
+        coef = {}
+
+        def stage2(b, r, ss):
+            k0, n = ranges[b][r]
+            bank = next_bank("vector", VECTOR_BANKS)
+            for i, s in enumerate(ss):
+                cols = slice(P * (s % 2), P * (s % 2 + 1))
+                for j in range(PASSES):
+                    nc.tensor.matmul_mx(
+                        out=bank[:, n * i : n * (i + 1)],
+                        lhsT=u_codes[b][s // 2][j][:, cols].bitcast(FP8X4),
+                        lhsT_scale=u_scales[b][s // 2][j][:, cols],
+                        rhs=we_sb[:, j, 2 * k0 : 2 * (k0 + n)].bitcast(FP4X4),
+                        rhs_scale=wes_sb[:, j, k0 : k0 + n],
+                        start=(j == 0),
+                        stop=(j == PASSES - 1),
+                    )
+                coef[(b, r, s)] = bank[:, n * i : n * (i + 1)]
+
+        def finish(b, r, ss):
+            k0, n = ranges[b][r]
+            for s in ss:
+                nc.vector.scalar_tensor_tensor(
+                    out=res[b][r][:, s, :], in0=coef[(b, r, s)], scalar=alpha[b][:, s : s + 1],
+                    in1=x_sb[b][:, s, k0 : k0 + n], op0=ALU.mult, op1=ALU.mult,
+                )
+
+        def store_res(b, r, s0, ns):
+            k0, n = ranges[b][r]
+            nc.sync.dma_start(
+                out=out_0[b].rearrange("(p s) k -> p s k", s=PACK)[:, s0 : s0 + ns, k0 : k0 + n],
+                in_=res[b][r][:, s0 : s0 + ns, :],
+            )
+
+        def round_res(b, r, copy):
+            copy(
+                out=res_bf[b][r][:].rearrange("p (c i t) -> p c t i", i=RUN, t=PACK),
+                in_=res[b][r][:].rearrange("p t (c i) -> p c t i", i=RUN),
+            )
+
+        def quantize_res(b, r):
+            k0, n = ranges[b][r]
+            nc.vector.quantize_mx(
+                out=res_codes[b][r][:].bitcast(FP8X4),
+                scales=res_scales[:, K * b + k0 : K * b + k0 + n],
+                in_=res_bf[b][r][:],
+            )
+
+        def store_codes(b, r):
+            k0, n = ranges[b][r]
+            nc.sync.dma_start(
+                out=out_1[0].rearrange("p m t -> p (m t)").bitcast(I32)[:, K * b + k0 : K * b + k0 + n],
+                in_=res_codes[b][r][:].bitcast(I32),
+            )
+
+        def store_scales(m0, n, queues):
+            for q in range(4):
+                queues[q % len(queues)].dma_start(
+                    out=out_2[0, 4 * q : 4 * q + 4, m0 : m0 + n].bitcast(I32),
+                    in_=res_scales[32 * q : 32 * q + 4, m0 : m0 + n].bitcast(I32),
+                )
+
+        both = slice(0, PASSES)
+
+        def stage1_group(c, j):
+            stage1(c, j, (0, 1))
+            stage1(c, j, (2, 3))
+            tanh(c, j, range(PACK))
+
+        def turn_pair(b, i):
+            for s in (2 * i, 2 * i + 1):
+                turn_h(b, s)
+                copy_ht(b, s)
+
+        deal_scales(0)
+        deal_scales(1)
+        turn_pair(0, 0)
+        quantize_h(0, both)
+        score_products(0, 0)
+        score_products(0, 1)
+        turn_pair(0, 1)
+        deal_words(0)
+        quantize_h(1, both)
+        deal_words(1)
+        stage1_group(0, 0)
+        stage1_group(0, 1)
+        score_products(0, 2)
+        score_products(0, 3)
+        turn_pair(1, 0)
+        make_u(0, 0, 0)
+        make_u(0, 0, 1)
+        score_mask(0)
+        quantize_u(0, 0, 0)
+        score_partial(0)
+        quantize_u(0, 0, 1)
+        quantize_h(2, both)
+        stage1_group(1, 0)
+        score_gather(0)
+        score_row_min(0)
+        stage1_group(1, 1)
+        score_spread_min(0)
+        turn_pair(1, 1)
+        make_u(0, 1, 0)
+        score_all_min(0)
+        score_exp(0)
+        quantize_u(0, 1, 0)
+        make_u(0, 1, 1)
+        quantize_h(3, both)
+        quantize_u(0, 1, 1)
+        stage1_group(2, 0)
+        score_total(0)
+        stage1_group(2, 1)
+        score_factor(0)
+        score_keep(0)
+        stage2(0, 0, (0,))
+        stage2(0, 0, (1,))
+        make_u(1, 0, 0)
+        score_alpha(0)
+        quantize_u(1, 0, 0)
+        finish(0, 0, (0,))
+        make_u(1, 0, 1)
+        finish(0, 0, (1,))
+        store_res(0, 0, 0, 2)
+        quantize_u(1, 0, 1)
+        stage1_group(3, 0)
+        stage2(0, 0, (2,))
+        stage2(0, 0, (3,))
+        stage1_group(3, 1)
+        finish(0, 0, (2, 3))
+        store_res(0, 0, 2, 2)
+        round_res(0, 0, nc.scalar.copy)
+        stage2(0, 1, (0,))
+        for s in range(PACK):
+            score_products(1, s)
+        make_u(1, 1, 0)
+        finish(0, 1, (0,))
+        quantize_u(1, 1, 0)
+        stage2(0, 1, (1,))
+        stage2(0, 1, (2,))
+        make_u(1, 1, 1)
+        score_mask(1)
+        quantize_u(1, 1, 1)
+        score_partial(1)
+        score_gather(1)
+        stage2(0, 1, (3,))
+        finish(0, 1, (1,))
+        store_res(0, 1, 0, 2)
+        score_row_min(1)
+        score_spread_min(1)
+        finish(0, 1, (2,))
+        score_all_min(1)
+        score_exp(1)
+        score_total(1)
+        finish(0, 1, (3,))
+        store_res(0, 1, 2, 2)
+        round_res(0, 1, nc.scalar.copy)
+        stage2(1, 0, (0,))
+        stage2(1, 0, (1,))
+        stage2(1, 0, (2,))
+        score_factor(1)
+        quantize_res(0, 0)
+        store_codes(0, 0)
+        score_keep(1)
+        score_alpha(1)
+        for s in range(PACK):
+            finish(1, 0, (s,))
+            store_res(1, 0, s, 1)
+            if s == 0:
+                stage2(1, 0, (3,))
+        round_res(1, 0, nc.scalar.copy)
+        stage2(1, 1, (0, 1))
+        stage2(1, 1, (2, 3))
+        quantize_res(0, 1)
+        store_codes(0, 1)
+        store_scales(0, K, [nc.sync])
+        stage2(1, 2, (0, 1))
+        finish(1, 1, (0, 1))
+        store_res(1, 1, 0, 2)
+        stage2(1, 2, (2, 3))
+        finish(1, 1, (2, 3))
+        store_res(1, 1, 2, 2)
+        round_res(1, 1, nc.scalar.copy)
+        finish(1, 2, (0, 1))
+        store_res(1, 2, 0, 2)
+        finish(1, 2, (2, 3))
+        store_res(1, 2, 2, 2)
+        quantize_res(1, 0)
+        store_codes(1, 0)
+        round_res(1, 2, nc.vector.tensor_copy)
+        quantize_res(1, 1)
+        store_codes(1, 1)
+        quantize_res(1, 2)
+        store_codes(1, 2)
+        store_scales(K, K, [nc.scalar, nc.sync])

@@ -75,16 +75,12 @@ def tile_retaincodecontributionmap_x2_kernel(
         h_scales = [sbuf("h_scales_%d" % c, [P, PASSES, P * ns], U8) for c, (b, s0, ns) in enumerate(chunks)]
         beta = [[sbuf("beta_%d_%d" % (c, j), [P, PACK, P * ns], F32) for j in range(PASSES)]
                 for c, (b, s0, ns) in enumerate(chunks)]
-        u_bf = [[[sbuf("u_%d_%d_%d" % (b, i, j), [P, 2 * P * PACK], BF16) for j in range(PASSES)] for i in range(2)]
-                for b in range(B)]
-        u_codes = [[[sbuf("uc_%d_%d_%d" % (b, i, j), [P, 2 * P], U32) for j in range(PASSES)] for i in range(2)]
-                   for b in range(B)]
-        u_scales = [[[sbuf("us_%d_%d_%d" % (b, i, j), [P, 2 * P], U8) for j in range(PASSES)] for i in range(2)]
-                    for b in range(B)]
-        ranges = [[(0, 512), (512, 512)], [(0, 512), (512, 256), (768, 256)]]
-        res = [[sbuf("res_%d_%d" % (b, k0), [P, PACK, n], F32) for (k0, n) in ranges[b]] for b in range(B)]
-        res_bf = [[sbuf("resbf_%d_%d" % (b, k0), [P, n * PACK], BF16) for (k0, n) in ranges[b]] for b in range(B)]
-        res_codes = [[sbuf("resc_%d_%d" % (b, k0), [P, n], U32) for (k0, n) in ranges[b]] for b in range(B)]
+        u_bf = [[sbuf("u_%d_%d" % (b, i), [P, PASSES, 2 * P * PACK], BF16) for i in range(2)] for b in range(B)]
+        u_codes = [[sbuf("uc_%d_%d" % (b, i), [P, PASSES, 2 * P], U32) for i in range(2)] for b in range(B)]
+        u_scales = [[sbuf("us_%d_%d" % (b, i), [P, PASSES, 2 * P], U8) for i in range(2)] for b in range(B)]
+        res = [[sbuf("res_%d_%d" % (b, r), [P, PACK, BANK], F32) for r in range(2)] for b in range(B)]
+        res_bf = {}
+        res_codes = [[sbuf("resc_%d_%d" % (b, r), [P, BANK], U32) for r in range(2)] for b in range(B)]
         res_scales = sbuf("res_scales", [P, B * K], U8)
         masked = [sbuf("masked_%d" % b, [P, 16, PACK], F32) for b in range(B)]
         part = [sbuf("part_%d" % b, [P, PACK, 4], F32) for b in range(B)]
@@ -95,11 +91,11 @@ def tile_retaincodecontributionmap_x2_kernel(
         row_sum = [sbuf("row_sum_%d" % b, [P, 1], F32) for b in range(B)]
         factor = [sbuf("factor_%d" % b, [P, 1], F32) for b in range(B)]
         alpha = [sbuf("alpha_%d" % b, [P, PACK], F32) for b in range(B)]
-        small = {0: ps.tile([P, BANK], F32, name="small", tag="small")}
+        small = {}
 
         def small_cols(b, c0, n):
             if b not in small:
-                small[b] = next_bank("scalar", SCALAR_BANKS)
+                small[b] = ps.tile([P, BANK], F32, name="small_%d" % b, tag="small")
             return small[b][:, c0 : c0 + n]
 
         def load_h(b, i):
@@ -126,9 +122,9 @@ def tile_retaincodecontributionmap_x2_kernel(
         make_identity(nc, ident[:])
         load_h(0, 0)
         load_h(0, 1)
+        load_h(0, 2)
         load_vec(wa_sb, wa)
         load_scale_rows(wbs_raw, wb_scales)
-        load_h(0, 2)
         load_wb(0)
         load_wb(1)
         load_vec(bb_sb, bb)
@@ -153,8 +149,8 @@ def tile_retaincodecontributionmap_x2_kernel(
                 in_=wbs_raw[:, :, BANK * j : BANK * (j + 1)].rearrange("p g (m t) -> p g t m", t=PACK),
             )
 
-        def deal_words(j):
-            nc.vector.tensor_copy(
+        def deal_words(j, copy):
+            copy(
                 out=wb_dealt[j][:].bitcast(U16).rearrange("p g (t m) -> p g t m", t=PACK),
                 in_=wb_raw[j][:].bitcast(U16).rearrange("p g (m t) -> p g t m", t=PACK),
             )
@@ -284,75 +280,79 @@ def tile_retaincodecontributionmap_x2_kernel(
             m0 = P * (2 * i - chunks[c][1])
             groups = 2 * P // RUN
             nc.vector.tensor_tensor(
-                out=u_bf[b][i][j][:].rearrange("p (c i t) -> p c t i", i=RUN, t=PACK),
+                out=u_bf[b][i][:, j, :].rearrange("p (c i t) -> p c t i", i=RUN, t=PACK),
                 in0=beta[c][j][:, :, m0 : m0 + 2 * P].rearrange("p t (c i) -> p c t i", i=RUN),
                 in1=wy_sb[:, j, :].unsqueeze(1).unsqueeze(3).to_broadcast([P, groups, PACK, RUN]),
                 op=ALU.mult,
             )
 
-        def quantize_u(b, i, j):
-            nc.vector.quantize_mx(out=u_codes[b][i][j][:].bitcast(FP8X4), scales=u_scales[b][i][j][:], in_=u_bf[b][i][j][:])
+        def quantize_u(b, i):
+            nc.vector.quantize_mx(
+                out=u_codes[b][i][:].rearrange("p j n -> p (j n)").bitcast(FP8X4),
+                scales=u_scales[b][i][:].rearrange("p j n -> p (j n)"),
+                in_=u_bf[b][i][:].rearrange("p j n -> p (j n)"),
+            )
 
         coef = {}
 
-        def stage2(b, r, ss):
-            k0, n = ranges[b][r]
-            bank = next_bank("vector", VECTOR_BANKS)
-            for i, s in enumerate(ss):
-                cols = slice(P * (s % 2), P * (s % 2 + 1))
-                for j in range(PASSES):
-                    nc.tensor.matmul_mx(
-                        out=bank[:, n * i : n * (i + 1)],
-                        lhsT=u_codes[b][s // 2][j][:, cols].bitcast(FP8X4),
-                        lhsT_scale=u_scales[b][s // 2][j][:, cols],
-                        rhs=we_sb[:, j, 2 * k0 : 2 * (k0 + n)].bitcast(FP4X4),
-                        rhs_scale=wes_sb[:, j, k0 : k0 + n],
-                        start=(j == 0),
-                        stop=(j == PASSES - 1),
-                    )
-                coef[(b, r, s)] = bank[:, n * i : n * (i + 1)]
-
-        def finish(b, r, ss):
-            k0, n = ranges[b][r]
-            for s in ss:
-                nc.vector.scalar_tensor_tensor(
-                    out=res[b][r][:, s, :], in0=coef[(b, r, s)], scalar=alpha[b][:, s : s + 1],
-                    in1=x_sb[b][:, s, k0 : k0 + n], op0=ALU.mult, op1=ALU.mult,
+        def stage2(b, r, s):
+            if len(coef) % (VECTOR_BANKS + SCALAR_BANKS) < VECTOR_BANKS:
+                bank = next_bank("vector", VECTOR_BANKS)
+            else:
+                bank = next_bank("scalar", SCALAR_BANKS)
+            cols = slice(P * (s % 2), P * (s % 2 + 1))
+            for j in range(PASSES):
+                nc.tensor.matmul_mx(
+                    out=bank[:],
+                    lhsT=u_codes[b][s // 2][:, j, cols].bitcast(FP8X4),
+                    lhsT_scale=u_scales[b][s // 2][:, j, cols],
+                    rhs=we_sb[:, j, 2 * BANK * r : 2 * BANK * (r + 1)].bitcast(FP4X4),
+                    rhs_scale=wes_sb[:, j, BANK * r : BANK * (r + 1)],
+                    start=(j == 0),
+                    stop=(j == PASSES - 1),
                 )
+            coef[(b, r, s)] = bank
+
+        def finish(b, r, s):
+            nc.vector.scalar_tensor_tensor(
+                out=res[b][r][:, s, :], in0=coef[(b, r, s)][:], scalar=alpha[b][:, s : s + 1],
+                in1=x_sb[b][:, s, BANK * r : BANK * (r + 1)], op0=ALU.mult, op1=ALU.mult,
+            )
 
         def store_res(b, r, s0, ns):
-            k0, n = ranges[b][r]
             nc.sync.dma_start(
-                out=out_0[b].rearrange("(p s) k -> p s k", s=PACK)[:, s0 : s0 + ns, k0 : k0 + n],
+                out=out_0[b].rearrange("(p s) k -> p s k", s=PACK)[:, s0 : s0 + ns, BANK * r : BANK * (r + 1)],
                 in_=res[b][r][:, s0 : s0 + ns, :],
             )
 
-        def round_res(b, r, copy):
+        def round_res(b, r, k0, n, copy):
+            res_bf[(b, r, k0)] = sbuf("resbf_%d_%d_%d" % (b, r, k0), [P, n * PACK], BF16)
             copy(
-                out=res_bf[b][r][:].rearrange("p (c i t) -> p c t i", i=RUN, t=PACK),
-                in_=res[b][r][:].rearrange("p t (c i) -> p c t i", i=RUN),
+                out=res_bf[(b, r, k0)][:].rearrange("p (c i t) -> p c t i", i=RUN, t=PACK),
+                in_=res[b][r][:, :, k0 : k0 + n].rearrange("p t (c i) -> p c t i", i=RUN),
             )
 
-        def quantize_res(b, r):
-            k0, n = ranges[b][r]
+        def quantize_res(b, r, k0, n):
+            m0 = K * b + BANK * r + k0
             nc.vector.quantize_mx(
-                out=res_codes[b][r][:].bitcast(FP8X4),
-                scales=res_scales[:, K * b + k0 : K * b + k0 + n],
-                in_=res_bf[b][r][:],
+                out=res_codes[b][r][:, k0 : k0 + n].bitcast(FP8X4),
+                scales=res_scales[:, m0 : m0 + n],
+                in_=res_bf[(b, r, k0)][:],
             )
 
         def store_codes(b, r):
-            k0, n = ranges[b][r]
+            m0 = K * b + BANK * r
             nc.sync.dma_start(
-                out=out_1[0].rearrange("p m t -> p (m t)").bitcast(I32)[:, K * b + k0 : K * b + k0 + n],
+                out=out_1[0].rearrange("p m t -> p (m t)").bitcast(I32)[:, m0 : m0 + BANK],
                 in_=res_codes[b][r][:].bitcast(I32),
             )
 
-        def store_scales(m0, n, queues):
+        def store_scales():
             for q in range(4):
-                queues[q % len(queues)].dma_start(
-                    out=out_2[0, 4 * q : 4 * q + 4, m0 : m0 + n].bitcast(I32),
-                    in_=res_scales[32 * q : 32 * q + 4, m0 : m0 + n].bitcast(I32),
+                queue = nc.scalar if q % 2 == 0 else nc.sync
+                queue.dma_start(
+                    out=out_2[0, 4 * q : 4 * q + 4, :].bitcast(I32),
+                    in_=res_scales[32 * q : 32 * q + 4, :].bitcast(I32),
                 )
 
         both = slice(0, PASSES)
@@ -367,123 +367,114 @@ def tile_retaincodecontributionmap_x2_kernel(
                 turn_h(b, s)
                 copy_ht(b, s)
 
-        deal_scales(0)
-        deal_scales(1)
         turn_pair(0, 0)
-        quantize_h(0, both)
-        score_products(0, 0)
-        score_products(0, 1)
         turn_pair(0, 1)
-        deal_words(0)
-        quantize_h(1, both)
-        deal_words(1)
-        stage1_group(0, 0)
-        stage1_group(0, 1)
-        score_products(0, 2)
-        score_products(0, 3)
-        turn_pair(1, 0)
-        make_u(0, 0, 0)
-        make_u(0, 0, 1)
+        quantize_h(0, both)
+        deal_scales(0)
+        deal_words(0, nc.vector.tensor_copy)
+        deal_words(1, nc.scalar.copy)
+        for s in range(PACK):
+            score_products(0, s)
+        deal_scales(1)
         score_mask(0)
-        quantize_u(0, 0, 0)
+        quantize_h(1, both)
         score_partial(0)
-        quantize_u(0, 0, 1)
-        quantize_h(2, both)
-        stage1_group(1, 0)
+        stage1_group(0, 0)
         score_gather(0)
         score_row_min(0)
-        stage1_group(1, 1)
+        stage1_group(0, 1)
         score_spread_min(0)
-        turn_pair(1, 1)
-        make_u(0, 1, 0)
+        turn_pair(1, 0)
+        make_u(0, 0, 0)
         score_all_min(0)
         score_exp(0)
-        quantize_u(0, 1, 0)
-        make_u(0, 1, 1)
-        quantize_h(3, both)
-        quantize_u(0, 1, 1)
-        stage1_group(2, 0)
+        make_u(0, 0, 1)
+        stage1_group(1, 0)
         score_total(0)
-        stage1_group(2, 1)
+        quantize_h(2, both)
+        quantize_u(0, 0)
         score_factor(0)
         score_keep(0)
-        stage2(0, 0, (0,))
-        stage2(0, 0, (1,))
-        make_u(1, 0, 0)
+        stage1_group(1, 1)
+        turn_pair(1, 1)
+        make_u(0, 1, 0)
         score_alpha(0)
-        quantize_u(1, 0, 0)
-        finish(0, 0, (0,))
-        make_u(1, 0, 1)
-        finish(0, 0, (1,))
-        store_res(0, 0, 0, 2)
-        quantize_u(1, 0, 1)
+        make_u(0, 1, 1)
+        quantize_h(3, both)
+        quantize_u(0, 1)
+        stage1_group(2, 0)
+        stage1_group(2, 1)
         stage1_group(3, 0)
-        stage2(0, 0, (2,))
-        stage2(0, 0, (3,))
         stage1_group(3, 1)
-        finish(0, 0, (2, 3))
-        store_res(0, 0, 2, 2)
-        round_res(0, 0, nc.scalar.copy)
-        stage2(0, 1, (0,))
-        for s in range(PACK):
-            score_products(1, s)
+        score_products(1, 0)
+        score_products(1, 1)
+        stage2(0, 0, 0)
+        score_products(1, 2)
+        score_products(1, 3)
+        for s in range(1, PACK):
+            stage2(0, 0, s)
+        make_u(1, 0, 0)
+        make_u(1, 0, 1)
         make_u(1, 1, 0)
-        finish(0, 1, (0,))
-        quantize_u(1, 1, 0)
-        stage2(0, 1, (1,))
-        stage2(0, 1, (2,))
+        quantize_u(1, 0)
         make_u(1, 1, 1)
         score_mask(1)
-        quantize_u(1, 1, 1)
+        finish(0, 0, 0)
         score_partial(1)
+        quantize_u(1, 1)
+        stage2(0, 1, 0)
         score_gather(1)
-        stage2(0, 1, (3,))
-        finish(0, 1, (1,))
-        store_res(0, 1, 0, 2)
+        stage2(0, 1, 1)
+        finish(0, 0, 1)
+        store_res(0, 0, 0, 2)
         score_row_min(1)
         score_spread_min(1)
-        finish(0, 1, (2,))
+        stage2(0, 1, 2)
+        stage2(0, 1, 3)
+        finish(0, 0, 2)
         score_all_min(1)
         score_exp(1)
+        finish(0, 0, 3)
+        store_res(0, 0, 2, 2)
+        round_res(0, 0, 0, BANK, nc.scalar.copy)
         score_total(1)
-        finish(0, 1, (3,))
-        store_res(0, 1, 2, 2)
-        round_res(0, 1, nc.scalar.copy)
-        stage2(1, 0, (0,))
-        stage2(1, 0, (1,))
-        stage2(1, 0, (2,))
+        stage2(1, 0, 0)
+        stage2(1, 0, 1)
+        finish(0, 1, 0)
+        stage2(1, 0, 2)
+        finish(0, 1, 1)
+        store_res(0, 1, 0, 2)
+        stage2(1, 0, 3)
         score_factor(1)
-        quantize_res(0, 0)
-        store_codes(0, 0)
+        finish(0, 1, 2)
         score_keep(1)
+        finish(0, 1, 3)
+        store_res(0, 1, 2, 2)
+        round_res(0, 1, 0, BANK, nc.scalar.copy)
         score_alpha(1)
+        quantize_res(0, 0, 0, BANK)
+        store_codes(0, 0)
+        for s in range(3):
+            stage2(1, 1, s)
         for s in range(PACK):
-            finish(1, 0, (s,))
-            store_res(1, 0, s, 1)
-            if s == 0:
-                stage2(1, 0, (3,))
-        round_res(1, 0, nc.scalar.copy)
-        stage2(1, 1, (0, 1))
-        stage2(1, 1, (2, 3))
-        quantize_res(0, 1)
+            finish(1, 0, s)
+            if s % 2 == 1:
+                store_res(1, 0, s - 1, 2)
+        round_res(1, 0, 0, BANK, nc.scalar.copy)
+        quantize_res(0, 1, 0, BANK)
         store_codes(0, 1)
-        store_scales(0, K, [nc.sync])
-        stage2(1, 2, (0, 1))
-        finish(1, 1, (0, 1))
-        store_res(1, 1, 0, 2)
-        stage2(1, 2, (2, 3))
-        finish(1, 1, (2, 3))
-        store_res(1, 1, 2, 2)
-        round_res(1, 1, nc.scalar.copy)
-        finish(1, 2, (0, 1))
-        store_res(1, 2, 0, 2)
-        finish(1, 2, (2, 3))
-        store_res(1, 2, 2, 2)
-        quantize_res(1, 0)
+        for s in range(PACK):
+            finish(1, 1, s)
+            if s == 0:
+                stage2(1, 1, 3)
+            if s % 2 == 1:
+                store_res(1, 1, s - 1, 2)
+        half = BANK // 2
+        round_res(1, 1, 0, half, nc.scalar.copy)
+        quantize_res(1, 0, 0, BANK)
         store_codes(1, 0)
-        round_res(1, 2, nc.vector.tensor_copy)
-        quantize_res(1, 1)
+        round_res(1, 1, half, half, nc.vector.tensor_copy)
+        quantize_res(1, 1, 0, half)
+        quantize_res(1, 1, half, half)
         store_codes(1, 1)
-        quantize_res(1, 2)
-        store_codes(1, 2)
-        store_scales(K, K, [nc.scalar, nc.sync])
+        store_scales()

@@ -95,16 +95,19 @@ def tile_retaincodecontributionmap_x2_kernel(
 
         def small_cols(b, c0, n):
             if b not in small:
-                small[b] = ps.tile([P, BANK], F32, name="small_%d" % b, tag="small")
+                if b == 0:
+                    small[b] = next_bank("vector", VECTOR_BANKS)
+                else:
+                    small[b] = ps.tile([P, BANK], F32, name="small", tag="small")
             return small[b][:, c0 : c0 + n]
 
         def load_h(b, i):
             s0, ns = h_loads[b][i]
             nc.sync.dma_start(out=h_sb[b][i][:], in_=h[b].rearrange("(p s) r -> p s r", s=PACK)[:, s0 : s0 + ns, :])
 
-        def load_scale_rows(dst, src):
+        def load_scale_rows(dst, src, queue):
             for q in range(4):
-                nc.sync.dma_start(
+                queue.dma_start(
                     out=dst[32 * q : 32 * q + 4, :, :].bitcast(I32),
                     in_=src[:, 4 * q : 4 * q + 4, :].rearrange("g r n -> r g n").bitcast(I32),
                 )
@@ -115,24 +118,24 @@ def tile_retaincodecontributionmap_x2_kernel(
                 in_=wb_words[:, :, 2 * BANK * j : 2 * BANK * (j + 1)].rearrange("g p n -> p g n").bitcast(I32),
             )
 
-        def load_vec(dst, src):
-            nc.sync.dma_start(out=dst[:], in_=src.rearrange("(g p t) -> p g t", g=PASSES, t=PACK))
+        def load_vec(dst, src, queue):
+            queue.dma_start(out=dst[:], in_=src.rearrange("(g p t) -> p g t", g=PASSES, t=PACK))
 
         nc.vector.memset(wbs_raw[:].bitcast(I32), 0)
         make_identity(nc, ident[:])
         load_h(0, 0)
         load_h(0, 1)
         load_h(0, 2)
-        load_vec(wa_sb, wa)
-        load_scale_rows(wbs_raw, wb_scales)
+        load_vec(wa_sb, wa, nc.scalar)
+        load_scale_rows(wbs_raw, wb_scales, nc.scalar)
         load_wb(0)
         load_wb(1)
-        load_vec(bb_sb, bb)
-        load_vec(wy_sb, wy)
+        load_vec(bb_sb, bb, nc.sync)
+        load_vec(wy_sb, wy, nc.sync)
         load_h(1, 0)
         load_h(1, 1)
         nc.sync.dma_start(out=we_sb[:].bitcast(I32), in_=wemb_words.rearrange("g p n -> p g n").bitcast(I32))
-        load_scale_rows(wes_sb, wemb_scales)
+        load_scale_rows(wes_sb, wemb_scales, nc.sync)
         for b in range(B):
             nc.sync.dma_start(out=x_sb[b][:], in_=x[b].rearrange("(p s) k -> p s k", s=PACK))
 
@@ -155,23 +158,35 @@ def tile_retaincodecontributionmap_x2_kernel(
                 in_=wb_raw[j][:].bitcast(U16).rearrange("p g (m t) -> p g t m", t=PACK),
             )
 
+        h_sorted = [sbuf("h_sorted_%d" % i, [P, 2, R // 2], F32) for i in range(2)]
+
+        def sort_words(i):
+            nc.vector.tensor_copy(
+                out=h_sorted[i][:].rearrange("p s (g u m) -> p (s g) u m", g=PASSES, u=2),
+                in_=h_sb[1][i][:].bitcast(F32).rearrange("p s (g m u) -> p (s g) u m", g=PASSES, u=2),
+            )
+
         turned = {}
 
         def turn_h(b, s):
             bank = next_bank("scalar", SCALAR_BANKS)
             i = [n for n, (s0, ns) in enumerate(h_loads[b]) if s0 <= s][-1]
-            words = h_sb[b][i][:, s - h_loads[b][i][0], :].bitcast(F32)
             for g in range(PASSES):
                 for u in range(2):
                     col = P * (2 * g + u)
-                    nc.tensor.transpose(bank[:, col : col + P], words[:, 256 * g + u : 256 * (g + 1) : 2], ident[:])
+                    if b == 0:
+                        words = h_sb[b][i][:, s - h_loads[b][i][0], :].bitcast(F32)
+                        src = words[:, 256 * g + u : 256 * (g + 1) : 2]
+                    else:
+                        src = h_sorted[i][:, s % 2, col : col + P]
+                    nc.tensor.transpose(bank[:, col : col + P], src, ident[:])
             turned[(b, s)] = bank
 
-        def copy_ht(b, s):
+        def copy_ht(b, s, copy):
             c = chunk_of(b, s)
             ls = s - chunks[c][1]
             dst = ht[c][:].bitcast(F32)[:, :, 2 * P * ls : 2 * P * (ls + 1)]
-            nc.scalar.copy(
+            copy(
                 out=dst.rearrange("p g (m u) -> p g m u", u=2),
                 in_=turned[(b, s)][:].rearrange("p (g u m) -> p g m u", g=PASSES, u=2),
             )
@@ -286,6 +301,15 @@ def tile_retaincodecontributionmap_x2_kernel(
                 op=ALU.mult,
             )
 
+        def make_u_gpsimd(b, i, j):
+            c = chunk_of(b, 2 * i)
+            nc.gpsimd.tensor_tensor(
+                out=u_bf[b][i][:, j, :].rearrange("p (n t) -> p n t", t=PACK),
+                in0=beta[c][j][:].rearrange("p t n -> p n t"),
+                in1=wy_sb[:, j, :].unsqueeze(1).to_broadcast([P, 2 * P, PACK]),
+                op=ALU.mult,
+            )
+
         def quantize_u(b, i):
             nc.vector.quantize_mx(
                 out=u_codes[b][i][:].rearrange("p j n -> p (j n)").bitcast(FP8X4),
@@ -340,11 +364,11 @@ def tile_retaincodecontributionmap_x2_kernel(
                 in_=res_bf[(b, r, k0)][:],
             )
 
-        def store_codes(b, r):
-            m0 = K * b + BANK * r
+        def store_codes(b, r, k0=0, n=BANK):
+            m0 = K * b + BANK * r + k0
             nc.sync.dma_start(
-                out=out_1[0].rearrange("p m t -> p (m t)").bitcast(I32)[:, m0 : m0 + BANK],
-                in_=res_codes[b][r][:].bitcast(I32),
+                out=out_1[0].rearrange("p m t -> p (m t)").bitcast(I32)[:, m0 : m0 + n],
+                in_=res_codes[b][r][:, k0 : k0 + n].bitcast(I32),
             )
 
         def store_scales():
@@ -365,108 +389,116 @@ def tile_retaincodecontributionmap_x2_kernel(
         def turn_pair(b, i):
             for s in (2 * i, 2 * i + 1):
                 turn_h(b, s)
-                copy_ht(b, s)
+                copy_ht(b, s, nc.scalar.copy)
 
         turn_pair(0, 0)
         turn_pair(0, 1)
-        quantize_h(0, both)
         deal_scales(0)
+        deal_scales(1)
+        quantize_h(0, both)
         deal_words(0, nc.vector.tensor_copy)
         deal_words(1, nc.scalar.copy)
-        for s in range(PACK):
-            score_products(0, s)
-        deal_scales(1)
-        score_mask(0)
+        score_products(0, 0)
+        score_products(0, 1)
+        stage1(0, 0, (0, 1))
+        score_products(0, 2)
+        score_products(0, 3)
+        stage1(0, 0, (2, 3))
+        tanh(0, 0, range(PACK))
         quantize_h(1, both)
+        sort_words(0)
+        score_mask(0)
+        sort_words(1)
         score_partial(0)
-        stage1_group(0, 0)
-        score_gather(0)
-        score_row_min(0)
         stage1_group(0, 1)
-        score_spread_min(0)
+        score_gather(0)
         turn_pair(1, 0)
         make_u(0, 0, 0)
-        score_all_min(0)
-        score_exp(0)
+        score_row_min(0)
         make_u(0, 0, 1)
         stage1_group(1, 0)
-        score_total(0)
         quantize_h(2, both)
         quantize_u(0, 0)
-        score_factor(0)
-        score_keep(0)
         stage1_group(1, 1)
+        score_spread_min(0)
         turn_pair(1, 1)
+        score_products(1, 0)
         make_u(0, 1, 0)
-        score_alpha(0)
+        score_all_min(0)
+        score_exp(0)
         make_u(0, 1, 1)
         quantize_h(3, both)
         quantize_u(0, 1)
         stage1_group(2, 0)
-        stage1_group(2, 1)
-        stage1_group(3, 0)
-        stage1_group(3, 1)
-        score_products(1, 0)
         score_products(1, 1)
-        stage2(0, 0, 0)
+        score_total(0)
+        stage1_group(2, 1)
         score_products(1, 2)
+        stage1_group(3, 0)
         score_products(1, 3)
-        for s in range(1, PACK):
-            stage2(0, 0, s)
+        stage1_group(3, 1)
+        stage2(0, 0, 0)
+        score_factor(0)
         make_u(1, 0, 0)
+        score_keep(0)
         make_u(1, 0, 1)
-        make_u(1, 1, 0)
-        quantize_u(1, 0)
-        make_u(1, 1, 1)
+        score_alpha(0)
         score_mask(1)
-        finish(0, 0, 0)
+        quantize_u(1, 0)
         score_partial(1)
-        quantize_u(1, 1)
-        stage2(0, 1, 0)
+        make_u(1, 1, 0)
+        make_u_gpsimd(1, 1, 1)
         score_gather(1)
-        stage2(0, 1, 1)
+        stage2(0, 0, 1)
+        finish(0, 0, 0)
+        score_row_min(1)
+        stage2(0, 0, 2)
+        score_spread_min(1)
+        stage2(0, 0, 3)
         finish(0, 0, 1)
         store_res(0, 0, 0, 2)
-        score_row_min(1)
-        score_spread_min(1)
-        stage2(0, 1, 2)
-        stage2(0, 1, 3)
         finish(0, 0, 2)
         score_all_min(1)
         score_exp(1)
+        stage2(0, 1, 0)
+        stage2(0, 1, 1)
+        score_total(1)
+        stage2(0, 1, 2)
+        stage2(0, 1, 3)
         finish(0, 0, 3)
         store_res(0, 0, 2, 2)
         round_res(0, 0, 0, BANK, nc.scalar.copy)
-        score_total(1)
         stage2(1, 0, 0)
         stage2(1, 0, 1)
         finish(0, 1, 0)
-        stage2(1, 0, 2)
         finish(0, 1, 1)
         store_res(0, 1, 0, 2)
-        stage2(1, 0, 3)
-        score_factor(1)
+        stage2(1, 1, 0)
         finish(0, 1, 2)
-        score_keep(1)
+        score_factor(1)
         finish(0, 1, 3)
         store_res(0, 1, 2, 2)
         round_res(0, 1, 0, BANK, nc.scalar.copy)
-        score_alpha(1)
+        quantize_u(1, 1)
+        score_keep(1)
         quantize_res(0, 0, 0, BANK)
         store_codes(0, 0)
-        for s in range(3):
-            stage2(1, 1, s)
+        score_alpha(1)
+        stage2(1, 0, 2)
+        stage2(1, 0, 3)
+        stage2(1, 1, 1)
         for s in range(PACK):
             finish(1, 0, s)
+            if s < 2:
+                stage2(1, 1, 2 + s)
             if s % 2 == 1:
                 store_res(1, 0, s - 1, 2)
         round_res(1, 0, 0, BANK, nc.scalar.copy)
+        finish(1, 1, 0)
         quantize_res(0, 1, 0, BANK)
         store_codes(0, 1)
-        for s in range(PACK):
+        for s in range(1, PACK):
             finish(1, 1, s)
-            if s == 0:
-                stage2(1, 1, 3)
             if s % 2 == 1:
                 store_res(1, 1, s - 1, 2)
         half = BANK // 2

@@ -79,7 +79,7 @@ def tile_retaincodecontributionmap_x2_kernel(
         u_codes = [[sbuf("uc_%d_%d" % (b, i), [P, PASSES, 2 * P], U32) for i in range(2)] for b in range(B)]
         u_scales = [[sbuf("us_%d_%d" % (b, i), [P, PASSES, 2 * P], U8) for i in range(2)] for b in range(B)]
         res = [[sbuf("res_%d_%d" % (b, r), [P, PACK, BANK], F32) for r in range(2)] for b in range(B)]
-        res_bf = {}
+        res_bf = [[sbuf("resbf_%d_%d" % (b, r), [P, BANK * PACK], BF16) for r in range(2)] for b in range(B)]
         res_codes = [[sbuf("resc_%d_%d" % (b, r), [P, BANK], U32) for r in range(2)] for b in range(B)]
         res_scales = sbuf("res_scales", [P, B * K], U8)
         masked = [sbuf("masked_%d" % b, [P, 16, PACK], F32) for b in range(B)]
@@ -126,9 +126,9 @@ def tile_retaincodecontributionmap_x2_kernel(
         load_h(0, 0)
         load_h(0, 1)
         load_h(0, 2)
-        load_vec(wa_sb, wa, nc.scalar)
-        load_scale_rows(wbs_raw, wb_scales, nc.scalar)
         load_wb(0)
+        load_vec(wa_sb, wa, nc.sync)
+        load_scale_rows(wbs_raw, wb_scales, nc.sync)
         load_wb(1)
         load_vec(bb_sb, bb, nc.sync)
         load_vec(wy_sb, wy, nc.sync)
@@ -146,16 +146,16 @@ def tile_retaincodecontributionmap_x2_kernel(
         nc.vector.tensor_copy(out=pick[:], in_=own_m[:].unsqueeze(1).to_broadcast([P, 4, 32]))
         nc.vector.tensor_scalar(out=neg_own_t[:], in0=own_t[:], scalar1=-1.0, scalar2=None, op0=ALU.mult)
 
-        def deal_scales(j):
+        def deal_scales(j, ts):
             nc.vector.tensor_copy(
-                out=wbs_dealt[j][:].rearrange("p g (t m) -> p g t m", t=PACK),
-                in_=wbs_raw[:, :, BANK * j : BANK * (j + 1)].rearrange("p g (m t) -> p g t m", t=PACK),
+                out=wbs_dealt[j][:].rearrange("p g (t m) -> p g t m", t=PACK)[:, :, ts, :],
+                in_=wbs_raw[:, :, BANK * j : BANK * (j + 1)].rearrange("p g (m t) -> p g t m", t=PACK)[:, :, ts, :],
             )
 
-        def deal_words(j, copy):
+        def deal_words(j, ts, copy):
             copy(
-                out=wb_dealt[j][:].bitcast(U16).rearrange("p g (t m) -> p g t m", t=PACK),
-                in_=wb_raw[j][:].bitcast(U16).rearrange("p g (m t) -> p g t m", t=PACK),
+                out=wb_dealt[j][:].bitcast(U16).rearrange("p g (t m) -> p g t m", t=PACK)[:, :, ts, :],
+                in_=wb_raw[j][:].bitcast(U16).rearrange("p g (m t) -> p g t m", t=PACK)[:, :, ts, :],
             )
 
         h_sorted = [sbuf("h_sorted_%d" % i, [P, 2, R // 2], F32) for i in range(2)]
@@ -343,6 +343,13 @@ def tile_retaincodecontributionmap_x2_kernel(
                 in1=x_sb[b][:, s, BANK * r : BANK * (r + 1)], op0=ALU.mult, op1=ALU.mult,
             )
 
+        def finish_beside(b, r, s):
+            scaled = sbuf("scaled_%d_%d_%d" % (b, r, s), [P, BANK], F32)
+            nc.scalar.activation(out=scaled[:], in_=coef[(b, r, s)][:], func=ACT.Copy, scale=alpha[b][:, s : s + 1])
+            nc.gpsimd.tensor_tensor(
+                out=res[b][r][:, s, :], in0=scaled[:], in1=x_sb[b][:, s, BANK * r : BANK * (r + 1)], op=ALU.mult
+            )
+
         def store_res(b, r, s0, ns):
             nc.sync.dma_start(
                 out=out_0[b].rearrange("(p s) k -> p s k", s=PACK)[:, s0 : s0 + ns, BANK * r : BANK * (r + 1)],
@@ -350,9 +357,8 @@ def tile_retaincodecontributionmap_x2_kernel(
             )
 
         def round_res(b, r, k0, n, copy):
-            res_bf[(b, r, k0)] = sbuf("resbf_%d_%d_%d" % (b, r, k0), [P, n * PACK], BF16)
             copy(
-                out=res_bf[(b, r, k0)][:].rearrange("p (c i t) -> p c t i", i=RUN, t=PACK),
+                out=res_bf[b][r][:, PACK * k0 : PACK * (k0 + n)].rearrange("p (c i t) -> p c t i", i=RUN, t=PACK),
                 in_=res[b][r][:, :, k0 : k0 + n].rearrange("p t (c i) -> p c t i", i=RUN),
             )
 
@@ -361,7 +367,7 @@ def tile_retaincodecontributionmap_x2_kernel(
             nc.vector.quantize_mx(
                 out=res_codes[b][r][:, k0 : k0 + n].bitcast(FP8X4),
                 scales=res_scales[:, m0 : m0 + n],
-                in_=res_bf[(b, r, k0)][:],
+                in_=res_bf[b][r][:, PACK * k0 : PACK * (k0 + n)],
             )
 
         def store_codes(b, r, k0=0, n=BANK):
@@ -393,14 +399,15 @@ def tile_retaincodecontributionmap_x2_kernel(
 
         turn_pair(0, 0)
         turn_pair(0, 1)
-        deal_scales(0)
-        deal_scales(1)
         quantize_h(0, both)
-        deal_words(0, nc.vector.tensor_copy)
-        deal_words(1, nc.scalar.copy)
+        for ts in (slice(0, 2), slice(2, 4)):
+            deal_words(0, ts, nc.vector.tensor_copy)
+            deal_scales(0, ts)
+        deal_scales(1, slice(0, 4))
+        deal_words(1, slice(0, 4), nc.scalar.copy)
         score_products(0, 0)
-        score_products(0, 1)
         stage1(0, 0, (0, 1))
+        score_products(0, 1)
         score_products(0, 2)
         score_products(0, 3)
         stage1(0, 0, (2, 3))
@@ -469,44 +476,45 @@ def tile_retaincodecontributionmap_x2_kernel(
         store_res(0, 0, 2, 2)
         round_res(0, 0, 0, BANK, nc.scalar.copy)
         stage2(1, 0, 0)
-        stage2(1, 0, 1)
+        stage2(1, 1, 0)
         finish(0, 1, 0)
+        score_factor(1)
         finish(0, 1, 1)
         store_res(0, 1, 0, 2)
-        stage2(1, 1, 0)
-        finish(0, 1, 2)
-        score_factor(1)
-        finish(0, 1, 3)
-        store_res(0, 1, 2, 2)
-        round_res(0, 1, 0, BANK, nc.scalar.copy)
-        quantize_u(1, 1)
         score_keep(1)
-        quantize_res(0, 0, 0, BANK)
-        store_codes(0, 0)
+        quantize_u(1, 1)
         score_alpha(1)
+        stage2(1, 0, 1)
+        finish(0, 1, 2)
+        store_res(0, 1, 2, 1)
         stage2(1, 0, 2)
+        finish(0, 1, 3)
+        store_res(0, 1, 3, 1)
+        finish_beside(1, 0, 0)
+        finish_beside(1, 1, 0)
+        round_res(0, 1, 0, BANK, nc.scalar.copy)
         stage2(1, 0, 3)
-        stage2(1, 1, 1)
-        for s in range(PACK):
+        for s in range(1, PACK):
+            stage2(1, 1, s)
             finish(1, 0, s)
-            if s < 2:
-                stage2(1, 1, 2 + s)
-            if s % 2 == 1:
-                store_res(1, 0, s - 1, 2)
+            if s == 1:
+                store_res(1, 0, 1, 1)
+        store_res(1, 0, 0, 1)
+        store_res(1, 0, 2, 2)
         round_res(1, 0, 0, BANK, nc.scalar.copy)
-        finish(1, 1, 0)
-        quantize_res(0, 1, 0, BANK)
-        store_codes(0, 1)
         for s in range(1, PACK):
             finish(1, 1, s)
-            if s % 2 == 1:
-                store_res(1, 1, s - 1, 2)
-        half = BANK // 2
-        round_res(1, 1, 0, half, nc.scalar.copy)
+            if s == 1:
+                store_res(1, 1, 1, 1)
+        store_res(1, 1, 0, 1)
+        store_res(1, 1, 2, 2)
+        for r in range(2):
+            quantize_res(0, r, 0, BANK)
+            store_codes(0, r)
+        round_res(1, 1, 0, 384, nc.vector.tensor_copy)
+        round_res(1, 1, 384, 128, nc.scalar.copy)
         quantize_res(1, 0, 0, BANK)
         store_codes(1, 0)
-        round_res(1, 1, half, half, nc.vector.tensor_copy)
-        quantize_res(1, 1, 0, half)
-        quantize_res(1, 1, half, half)
+        quantize_res(1, 1, 0, BANK)
         store_codes(1, 1)
         store_scales()

@@ -122,6 +122,15 @@ def tile_retaincodecontributionmap_x2_kernel(
             queue.dma_start(out=dst[:], in_=src.rearrange("(g p t) -> p g t", g=PASSES, t=PACK))
 
         nc.vector.memset(wbs_raw[:].bitcast(I32), 0)
+        warm = sbuf("warm", [P, BANK], BF16)
+        nc.vector.memset(warm[:], 0.0)
+        warm_bank = ps.tile([P, BANK], F32, name="warm_bank", tag="small")
+
+        def warm_up(n):
+            for i in range(n):
+                nc.tensor.matmul(warm_bank[:], lhsT=warm[:, 0:P], rhs=warm[:], start=True, stop=True)
+
+        warm_up(3)
         make_identity(nc, ident[:])
         load_h(0, 0)
         load_h(0, 1)
@@ -398,7 +407,9 @@ def tile_retaincodecontributionmap_x2_kernel(
                 copy_ht(b, s, nc.scalar.copy)
 
         turn_pair(0, 0)
+        warm_up(2)
         turn_pair(0, 1)
+        warm_up(1)
         quantize_h(0, both)
         for ts in (slice(0, 2), slice(2, 4)):
             deal_words(0, ts, nc.vector.tensor_copy)

from contextlib import ExitStack

import concourse.mybir as mybir
from concourse.masks import make_identity

B, T, R, D, K = 2, 512, 1024, 1024, 1024
FLOPS = 2 * B * T * R * D + 2 * B * T * D * K + 2 * B * T * R

F32 = mybir.dt.float32
BF16 = mybir.dt.bfloat16
I32 = mybir.dt.int32
U32 = mybir.dt.uint32
U16 = mybir.dt.uint16
U8 = mybir.dt.uint8
FP8X4 = mybir.dt.float8_e4m3fn_x4
FP4X4 = mybir.dt.float4_e2m1fn_x4
ALU = mybir.AluOpType
ACT = mybir.ActivationFunctionType
AX = mybir.AxisListType

P = 128
PACK = 4
PASSES = 2
BANK = 512
SCALAR_BANKS = 4
VECTOR_BANKS = 3
RUN = 4


def tile_retaincodecontributionmap_x2_kernel(
    tc, h, wa, wb_words, wb_scales, bb, wy, wemb_words, wemb_scales, x, out_0, out_1, out_2
):
    nc = tc.nc
    with ExitStack() as ctx:
        sb = ctx.enter_context(tc.tile_pool(name="sb", bufs=1))
        ps = ctx.enter_context(tc.psum_pool(name="ps", bufs=1))
        ctx.enter_context(tc.manual_schedule())

        def sbuf(name, shape, dtype):
            return sb.tile(shape, dtype, name=name, align_bytes=256)

        bank_count = {"scalar": 0, "vector": 0}

        def next_bank(reader, banks):
            n = bank_count[reader]
            bank_count[reader] = n + 1
            return ps.tile([P, BANK], F32, name="%s_bank_%d" % (reader, n), tag="%s_bank_%d" % (reader, n % banks))

        chunks = [(0, 0, 2), (0, 2, 2), (1, 0, 2), (1, 2, 2)]

        def chunk_of(b, s):
            return [c for c, (cb, s0, ns) in enumerate(chunks) if cb == b and s0 <= s < s0 + ns][0]

        ident = sbuf("ident", [P, P], F32)
        own_m = sbuf("own_m", [P, 32], F32)
        pick = sbuf("pick", [P, 4, 32], F32)
        own_q = sbuf("own_q", [P, 4], F32)
        own_t = sbuf("own_t", [P, PACK], F32)
        neg_own_t = sbuf("neg_own_t", [P, PACK], F32)
        inv_visits = sbuf("inv_visits", [P, 2], F32)
        h_loads = [[(0, 1), (1, 1), (2, 2)], [(0, 2), (2, 2)]]
        h_sb = [[sbuf("h_%d_%d" % (b, s0), [P, ns, R], BF16) for (s0, ns) in h_loads[b]] for b in range(B)]
        x_sb = [sbuf("x_%d" % b, [P, PACK, K], BF16) for b in range(B)]
        wb_raw = [sbuf("wb_raw_%d" % j, [P, PASSES, 2 * BANK], U8) for j in range(PASSES)]
        wb_dealt = [sbuf("wb_dealt_%d" % j, [P, PASSES, 2 * BANK], U8) for j in range(PASSES)]
        wbs_raw = sbuf("wbs_raw", [P, PASSES, D], U8)
        wbs_dealt = [sbuf("wbs_dealt_%d" % j, [P, PASSES, BANK], U8) for j in range(PASSES)]
        we_sb = sbuf("we_sb", [P, PASSES, 2 * K], U8)
        wes_sb = sbuf("wes_sb", [P, PASSES, K], U8)
        wa_sb = sbuf("wa_sb", [P, PASSES, PACK], BF16)
        bb_sb = sbuf("bb_sb", [P, PASSES, PACK], BF16)
        wy_sb = sbuf("wy_sb", [P, PASSES, PACK], BF16)
        ht = [sbuf("ht_%d" % c, [P, PASSES, P * ns * PACK], BF16) for c, (b, s0, ns) in enumerate(chunks)]
        h_codes = [sbuf("h_codes_%d" % c, [P, PASSES, P * ns], U32) for c, (b, s0, ns) in enumerate(chunks)]
        h_scales = [sbuf("h_scales_%d" % c, [P, PASSES, P * ns], U8) for c, (b, s0, ns) in enumerate(chunks)]
        beta = [[sbuf("beta_%d_%d" % (c, j), [P, PACK, P * ns], F32) for j in range(PASSES)]
                for c, (b, s0, ns) in enumerate(chunks)]
        u_bf = [[sbuf("u_%d_%d" % (b, i), [P, PASSES, 2 * P * PACK], BF16) for i in range(2)] for b in range(B)]
        u_codes = [[sbuf("uc_%d_%d" % (b, i), [P, PASSES, 2 * P], U32) for i in range(2)] for b in range(B)]
        u_scales = [[sbuf("us_%d_%d" % (b, i), [P, PASSES, 2 * P], U8) for i in range(2)] for b in range(B)]
        res = [[sbuf("res_%d_%d" % (b, r), [P, PACK, BANK], F32) for r in range(2)] for b in range(B)]
        res_bf = [[sbuf("resbf_%d_%d" % (b, r), [P, BANK * PACK], BF16) for r in range(2)] for b in range(B)]
        res_codes = [[sbuf("resc_%d_%d" % (b, r), [P, BANK], U32) for r in range(2)] for b in range(B)]
        res_scales = sbuf("res_scales", [P, B * K], U8)
        masked = [sbuf("masked_%d" % b, [P, 16, PACK], F32) for b in range(B)]
        part = [sbuf("part_%d" % b, [P, PACK, 4], F32) for b in range(B)]
        row_min = [sbuf("row_min_%d" % b, [P, 1], F32) for b in range(B)]
        all_min = [sbuf("all_min_%d" % b, [P, 1], F32) for b in range(B)]
        expo = [sbuf("expo_%d" % b, [P, PACK, 4], F32) for b in range(B)]
        kept = [sbuf("kept_%d" % b, [P, PACK, 4], F32) for b in range(B)]
        row_sum = [sbuf("row_sum_%d" % b, [P, 1], F32) for b in range(B)]
        factor = [sbuf("factor_%d" % b, [P, 1], F32) for b in range(B)]
        alpha = [sbuf("alpha_%d" % b, [P, PACK], F32) for b in range(B)]
        small = {}

        def small_cols(b, c0, n):
            if b not in small:
                if b == 0:
                    small[b] = next_bank("vector", VECTOR_BANKS)
                else:
                    small[b] = ps.tile([P, BANK], F32, name="small", tag="small")
            return small[b][:, c0 : c0 + n]

        def load_h(b, i):
            s0, ns = h_loads[b][i]
            nc.sync.dma_start(out=h_sb[b][i][:], in_=h[b].rearrange("(p s) r -> p s r", s=PACK)[:, s0 : s0 + ns, :])

        def load_scale_rows(dst, src, queue):
            for q in range(4):
                queue.dma_start(
                    out=dst[32 * q : 32 * q + 4, :, :].bitcast(I32),
                    in_=src[:, 4 * q : 4 * q + 4, :].rearrange("g r n -> r g n").bitcast(I32),
                )

        def load_wb(j):
            nc.sync.dma_start(
                out=wb_raw[j][:].bitcast(I32),
                in_=wb_words[:, :, 2 * BANK * j : 2 * BANK * (j + 1)].rearrange("g p n -> p g n").bitcast(I32),
            )

        def load_vec(dst, src, queue):
            queue.dma_start(out=dst[:], in_=src.rearrange("(g p t) -> p g t", g=PASSES, t=PACK))

        nc.vector.memset(wbs_raw[:].bitcast(I32), 0)
        warm = sbuf("warm", [P, BANK], BF16)
        nc.vector.memset(warm[:], 0.0)
        warm_bank = ps.tile([P, BANK], F32, name="warm_bank", tag="small")

        def warm_up(n):
            for i in range(n):
                nc.tensor.matmul(warm_bank[:], lhsT=warm[:, 0:P], rhs=warm[:], start=True, stop=True)

        warm_up(3)
        make_identity(nc, ident[:])
        load_h(0, 0)
        load_h(0, 1)
        load_h(0, 2)
        load_wb(0)
        load_vec(wa_sb, wa, nc.sync)
        load_scale_rows(wbs_raw, wb_scales, nc.sync)
        load_wb(1)
        load_vec(bb_sb, bb, nc.sync)
        load_vec(wy_sb, wy, nc.sync)
        load_h(1, 0)
        load_h(1, 1)
        nc.sync.dma_start(out=we_sb[:].bitcast(I32), in_=wemb_words.rearrange("g p n -> p g n").bitcast(I32))
        load_scale_rows(wes_sb, wemb_scales, nc.sync)
        for b in range(B):
            nc.sync.dma_start(out=x_sb[b][:], in_=x[b].rearrange("(p s) k -> p s k", s=PACK))

        nc.vector.memset(inv_visits[:], 1.0 / (4 * T))
        nc.vector.tensor_reduce(out=own_t[:], in_=ident[:].rearrange("p (m t) -> p t m", t=PACK), axis=AX.X, op=ALU.add)
        nc.vector.tensor_reduce(out=own_m[:], in_=ident[:].rearrange("p (m t) -> p m t", t=PACK), axis=AX.X, op=ALU.add)
        nc.vector.tensor_reduce(out=own_q[:], in_=ident[:].rearrange("p (q m) -> p q m", q=4), axis=AX.X, op=ALU.add)
        nc.vector.tensor_copy(out=pick[:], in_=own_m[:].unsqueeze(1).to_broadcast([P, 4, 32]))
        nc.vector.tensor_scalar(out=neg_own_t[:], in0=own_t[:], scalar1=-1.0, scalar2=None, op0=ALU.mult)

        def deal_scales(j, ts):
            nc.vector.tensor_copy(
                out=wbs_dealt[j][:].rearrange("p g (t m) -> p g t m", t=PACK)[:, :, ts, :],
                in_=wbs_raw[:, :, BANK * j : BANK * (j + 1)].rearrange("p g (m t) -> p g t m", t=PACK)[:, :, ts, :],
            )

        def deal_words(j, ts, copy):
            copy(
                out=wb_dealt[j][:].bitcast(U16).rearrange("p g (t m) -> p g t m", t=PACK)[:, :, ts, :],
                in_=wb_raw[j][:].bitcast(U16).rearrange("p g (m t) -> p g t m", t=PACK)[:, :, ts, :],
            )

        h_sorted = [sbuf("h_sorted_%d" % i, [P, 2, R // 2], F32) for i in range(2)]

        def sort_words(i):
            nc.vector.tensor_copy(
                out=h_sorted[i][:].rearrange("p s (g u m) -> p (s g) u m", g=PASSES, u=2),
                in_=h_sb[1][i][:].bitcast(F32).rearrange("p s (g m u) -> p (s g) u m", g=PASSES, u=2),
            )

        turned = {}

        def turn_h(b, s):
            bank = next_bank("scalar", SCALAR_BANKS)
            i = [n for n, (s0, ns) in enumerate(h_loads[b]) if s0 <= s][-1]
            for g in range(PASSES):
                for u in range(2):
                    col = P * (2 * g + u)
                    if b == 0:
                        words = h_sb[b][i][:, s - h_loads[b][i][0], :].bitcast(F32)
                        src = words[:, 256 * g + u : 256 * (g + 1) : 2]
                    else:
                        src = h_sorted[i][:, s % 2, col : col + P]
                    nc.tensor.transpose(bank[:, col : col + P], src, ident[:])
            turned[(b, s)] = bank

        def copy_ht(b, s, copy):
            c = chunk_of(b, s)
            ls = s - chunks[c][1]
            dst = ht[c][:].bitcast(F32)[:, :, 2 * P * ls : 2 * P * (ls + 1)]
            copy(
                out=dst.rearrange("p g (m u) -> p g m u", u=2),
                in_=turned[(b, s)][:].rearrange("p (g u m) -> p g m u", g=PASSES, u=2),
            )

        def quantize_h(c, gs):
            nc.vector.quantize_mx(
                out=h_codes[c][:, gs, :].rearrange("p g n -> p (g n)").bitcast(FP8X4),
                scales=h_scales[c][:, gs, :].rearrange("p g n -> p (g n)"),
                in_=ht[c][:, gs, :].rearrange("p g n -> p (g n)"),
            )

        def score_products(b, s):
            c = chunk_of(b, s)
            ls = s - chunks[c][1]
            for q in range(4):
                for g in range(PASSES):
                    col = P * (4 * ls + q)
                    nc.tensor.matmul(
                        small_cols(b, 16 * s + 4 * q, PACK),
                        lhsT=ht[c][:, g, col : col + P],
                        rhs=wa_sb[:, g, :],
                        start=(g == 0),
                        stop=(g == PASSES - 1),
                    )

        def score_mask(b):
            nc.vector.tensor_tensor(
                out=masked[b][:],
                in0=small_cols(b, 0, 64).rearrange("p (c t) -> p c t", t=PACK),
                in1=neg_own_t[:].unsqueeze(1).to_broadcast([P, 16, PACK]),
                op=ALU.mult,
            )

        def score_partial(b):
            nc.vector.tensor_reduce(
                out=part[b][:].rearrange("p s q -> p (s q)"), in_=masked[b][:], axis=AX.X, op=ALU.add
            )

        def score_gather(b):
            nc.tensor.matmul(
                small_cols(b, 64, 16),
                lhsT=pick[:].rearrange("p q m -> p (q m)"),
                rhs=part[b][:].rearrange("p s q -> p (s q)"),
                start=True,
                stop=True,
            )

        def score_row_min(b):
            nc.vector.tensor_reduce(out=row_min[b][:], in_=small_cols(b, 64, 16), axis=AX.X, op=ALU.min)

        def score_spread_min(b):
            nc.tensor.transpose(small_cols(b, 128, P), row_min[b][:].to_broadcast([P, P]), ident[:])

        def score_all_min(b):
            nc.vector.tensor_reduce(out=all_min[b][:], in_=small_cols(b, 128, P), axis=AX.X, op=ALU.min)

        def score_exp(b):
            nc.scalar.activation(
                out=expo[b][:].rearrange("p s q -> p (s q)"), in_=small_cols(b, 64, 16), func=ACT.Exp, bias=all_min[b][:], scale=-1.0,
                accum_out=row_sum[b][:],
            )

        def score_total(b):
            nc.tensor.matmul(
                small_cols(b, 80, 2), lhsT=row_sum[b][:].to_broadcast([P, P]), rhs=inv_visits[:], start=True, stop=True
            )

        def score_factor(b):
            nc.vector.reciprocal(out=factor[b][:], in_=small_cols(b, 80, 1))

        def score_keep(b):
            nc.vector.scalar_tensor_tensor(
                out=kept[b][:], in0=expo[b][:], scalar=factor[b][:],
                in1=own_q[:].unsqueeze(1).to_broadcast([P, PACK, 4]), op0=ALU.mult, op1=ALU.mult,
            )

        def score_alpha(b):
            nc.vector.tensor_reduce(out=alpha[b][:], in_=kept[b][:], axis=AX.X, op=ALU.add)

        pre = {}

        def stage1(c, j, ts):
            n = h_codes[c].shape[2]
            bank = next_bank("scalar", SCALAR_BANKS)
            for i, t in enumerate(ts):
                for g in range(PASSES):
                    nc.tensor.matmul_mx(
                        out=bank[:, n * i : n * (i + 1)],
                        lhsT=wb_dealt[j][:, g, 2 * P * t : 2 * P * (t + 1)].bitcast(FP4X4),
                        lhsT_scale=wbs_dealt[j][:, g, P * t : P * (t + 1)],
                        rhs=h_codes[c][:, g, :].bitcast(FP8X4),
                        rhs_scale=h_scales[c][:, g, :],
                        start=(g == 0),
                        stop=(g == PASSES - 1),
                    )
                pre[(c, j, t)] = bank[:, n * i : n * (i + 1)]

        def tanh(c, j, ts):
            for t in ts:
                nc.scalar.activation(
                    out=beta[c][j][:, t, :], in_=pre[(c, j, t)], func=ACT.Tanh, bias=bb_sb[:, j, t : t + 1]
                )

        def make_u(b, i, j):
            c = chunk_of(b, 2 * i)
            m0 = P * (2 * i - chunks[c][1])
            groups = 2 * P // RUN
            nc.vector.tensor_tensor(
                out=u_bf[b][i][:, j, :].rearrange("p (c i t) -> p c t i", i=RUN, t=PACK),
                in0=beta[c][j][:, :, m0 : m0 + 2 * P].rearrange("p t (c i) -> p c t i", i=RUN),
                in1=wy_sb[:, j, :].unsqueeze(1).unsqueeze(3).to_broadcast([P, groups, PACK, RUN]),
                op=ALU.mult,
            )

        def make_u_gpsimd(b, i, j):
            c = chunk_of(b, 2 * i)
            nc.gpsimd.tensor_tensor(
                out=u_bf[b][i][:, j, :].rearrange("p (n t) -> p n t", t=PACK),
                in0=beta[c][j][:].rearrange("p t n -> p n t"),
                in1=wy_sb[:, j, :].unsqueeze(1).to_broadcast([P, 2 * P, PACK]),
                op=ALU.mult,
            )

        def quantize_u(b, i):
            nc.vector.quantize_mx(
                out=u_codes[b][i][:].rearrange("p j n -> p (j n)").bitcast(FP8X4),
                scales=u_scales[b][i][:].rearrange("p j n -> p (j n)"),
                in_=u_bf[b][i][:].rearrange("p j n -> p (j n)"),
            )

        coef = {}

        def stage2(b, r, s):
            if len(coef) % (VECTOR_BANKS + SCALAR_BANKS) < VECTOR_BANKS:
                bank = next_bank("vector", VECTOR_BANKS)
            else:
                bank = next_bank("scalar", SCALAR_BANKS)
            cols = slice(P * (s % 2), P * (s % 2 + 1))
            for j in range(PASSES):
                nc.tensor.matmul_mx(
                    out=bank[:],
                    lhsT=u_codes[b][s // 2][:, j, cols].bitcast(FP8X4),
                    lhsT_scale=u_scales[b][s // 2][:, j, cols],
                    rhs=we_sb[:, j, 2 * BANK * r : 2 * BANK * (r + 1)].bitcast(FP4X4),
                    rhs_scale=wes_sb[:, j, BANK * r : BANK * (r + 1)],
                    start=(j == 0),
                    stop=(j == PASSES - 1),
                )
            coef[(b, r, s)] = bank

        def finish(b, r, s):
            nc.vector.scalar_tensor_tensor(
                out=res[b][r][:, s, :], in0=coef[(b, r, s)][:], scalar=alpha[b][:, s : s + 1],
                in1=x_sb[b][:, s, BANK * r : BANK * (r + 1)], op0=ALU.mult, op1=ALU.mult,
            )

        def finish_beside(b, r, s):
            scaled = sbuf("scaled_%d_%d_%d" % (b, r, s), [P, BANK], F32)
            nc.scalar.activation(out=scaled[:], in_=coef[(b, r, s)][:], func=ACT.Copy, scale=alpha[b][:, s : s + 1])
            nc.gpsimd.tensor_tensor(
                out=res[b][r][:, s, :], in0=scaled[:], in1=x_sb[b][:, s, BANK * r : BANK * (r + 1)], op=ALU.mult
            )

        def store_res(b, r, s0, ns):
            nc.sync.dma_start(
                out=out_0[b].rearrange("(p s) k -> p s k", s=PACK)[:, s0 : s0 + ns, BANK * r : BANK * (r + 1)],
                in_=res[b][r][:, s0 : s0 + ns, :],
            )

        def round_res(b, r, k0, n, copy):
            copy(
                out=res_bf[b][r][:, PACK * k0 : PACK * (k0 + n)].rearrange("p (c i t) -> p c t i", i=RUN, t=PACK),
                in_=res[b][r][:, :, k0 : k0 + n].rearrange("p t (c i) -> p c t i", i=RUN),
            )

        def quantize_res(b, r, k0, n):
            m0 = K * b + BANK * r + k0
            nc.vector.quantize_mx(
                out=res_codes[b][r][:, k0 : k0 + n].bitcast(FP8X4),
                scales=res_scales[:, m0 : m0 + n],
                in_=res_bf[b][r][:, PACK * k0 : PACK * (k0 + n)],
            )

        def store_codes(b, r, k0=0, n=BANK):
            m0 = K * b + BANK * r + k0
            nc.sync.dma_start(
                out=out_1[0].rearrange("p m t -> p (m t)").bitcast(I32)[:, m0 : m0 + n],
                in_=res_codes[b][r][:, k0 : k0 + n].bitcast(I32),
            )

        def store_scales():
            for q in range(4):
                queue = nc.scalar if q % 2 == 0 else nc.sync
                queue.dma_start(
                    out=out_2[0, 4 * q : 4 * q + 4, :].bitcast(I32),
                    in_=res_scales[32 * q : 32 * q + 4, :].bitcast(I32),
                )

        both = slice(0, PASSES)

        def stage1_group(c, j):
            stage1(c, j, (0, 1))
            stage1(c, j, (2, 3))
            tanh(c, j, range(PACK))

        def turn_pair(b, i):
            for s in (2 * i, 2 * i + 1):
                turn_h(b, s)
                copy_ht(b, s, nc.scalar.copy)

        turn_pair(0, 0)
        warm_up(2)
        turn_pair(0, 1)
        warm_up(1)
        quantize_h(0, both)
        for ts in (slice(0, 2), slice(2, 4)):
            deal_words(0, ts, nc.vector.tensor_copy)
            deal_scales(0, ts)
        deal_scales(1, slice(0, 4))
        deal_words(1, slice(0, 4), nc.scalar.copy)
        score_products(0, 0)
        stage1(0, 0, (0, 1))
        score_products(0, 1)
        score_products(0, 2)
        score_products(0, 3)
        stage1(0, 0, (2, 3))
        tanh(0, 0, range(PACK))
        quantize_h(1, both)
        sort_words(0)
        score_mask(0)
        sort_words(1)
        score_partial(0)
        stage1_group(0, 1)
        score_gather(0)
        turn_pair(1, 0)
        make_u(0, 0, 0)
        score_row_min(0)
        make_u(0, 0, 1)
        stage1_group(1, 0)
        quantize_h(2, both)
        quantize_u(0, 0)
        stage1_group(1, 1)
        score_spread_min(0)
        turn_pair(1, 1)
        score_products(1, 0)
        make_u(0, 1, 0)
        score_all_min(0)
        score_exp(0)
        make_u(0, 1, 1)
        quantize_h(3, both)
        quantize_u(0, 1)
        stage1_group(2, 0)
        score_products(1, 1)
        score_total(0)
        stage1_group(2, 1)
        score_products(1, 2)
        stage1_group(3, 0)
        score_products(1, 3)
        stage1_group(3, 1)
        stage2(0, 0, 0)
        score_factor(0)
        make_u(1, 0, 0)
        score_keep(0)
        make_u(1, 0, 1)
        score_alpha(0)
        score_mask(1)
        quantize_u(1, 0)
        score_partial(1)
        make_u(1, 1, 0)
        make_u_gpsimd(1, 1, 1)
        score_gather(1)
        stage2(0, 0, 1)
        finish(0, 0, 0)
        score_row_min(1)
        stage2(0, 0, 2)
        score_spread_min(1)
        stage2(0, 0, 3)
        finish(0, 0, 1)
        store_res(0, 0, 0, 2)
        finish(0, 0, 2)
        score_all_min(1)
        score_exp(1)
        stage2(0, 1, 0)
        stage2(0, 1, 1)
        score_total(1)
        stage2(0, 1, 2)
        stage2(0, 1, 3)
        finish(0, 0, 3)
        store_res(0, 0, 2, 2)
        round_res(0, 0, 0, BANK, nc.scalar.copy)
        stage2(1, 0, 0)
        stage2(1, 1, 0)
        finish(0, 1, 0)
        score_factor(1)
        finish(0, 1, 1)
        store_res(0, 1, 0, 2)
        score_keep(1)
        quantize_u(1, 1)
        score_alpha(1)
        stage2(1, 0, 1)
        finish(0, 1, 2)
        store_res(0, 1, 2, 1)
        stage2(1, 0, 2)
        finish(0, 1, 3)
        store_res(0, 1, 3, 1)
        finish_beside(1, 0, 0)
        finish_beside(1, 1, 0)
        round_res(0, 1, 0, BANK, nc.scalar.copy)
        stage2(1, 0, 3)
        for s in range(1, PACK):
            stage2(1, 1, s)
            finish(1, 0, s)
            if s == 1:
                store_res(1, 0, 1, 1)
        store_res(1, 0, 0, 1)
        store_res(1, 0, 2, 2)
        round_res(1, 0, 0, BANK, nc.scalar.copy)
        for s in range(1, PACK):
            finish(1, 1, s)
            if s == 1:
                store_res(1, 1, 1, 1)
        store_res(1, 1, 0, 1)
        store_res(1, 1, 2, 2)
        for r in range(2):
            quantize_res(0, r, 0, BANK)
            store_codes(0, r)
        round_res(1, 1, 0, 384, nc.vector.tensor_copy)
        round_res(1, 1, 384, 128, nc.scalar.copy)
        quantize_res(1, 0, 0, BANK)
        store_codes(1, 0)
        quantize_res(1, 1, 0, BANK)
        store_codes(1, 1)
        store_scales()
